import numpy as np
import ml_dtypes


def mxq(x, axis, fmt="e4m3"):
    dtype, down = {"e4m3": (ml_dtypes.float8_e4m3fn, 7), "e5m2": (ml_dtypes.float8_e5m2, 14)}[fmt]
    v = np.moveaxis(np.asarray(x, np.float32).astype(ml_dtypes.bfloat16).astype(np.float64), axis, -1)
    blocks = v.reshape(v.shape[:-1] + (-1, 32))
    amax = np.abs(blocks).max(-1, keepdims=True)
    byte = np.maximum(np.where(amax > 0, np.frexp(amax)[1] - 1 + 127, 0) - down, 1)
    scale = np.exp2(byte - 127.0)
    codes = (blocks / scale).astype(np.float32).astype(dtype).astype(np.float64)
    return np.moveaxis((codes * scale).reshape(v.shape), -1, axis)


WIDE = False


def mx_kscale(k):
    if not WIDE:
        return np.ones(k)
    levels = np.array([10, -10, 5, -5, 0])
    if k % 512:
        return np.exp2(np.random.permutation(np.resize(levels, k // 32))).repeat(32)
    a = np.empty((k // 512, 16))
    for p in range(k // 512):
        a[p, :8] = np.random.permutation(np.resize(levels, 8))
        for g in range(8):
            far = levels[np.abs(levels - a[p, g]) >= 10]
            a[p, g + 8] = far[np.random.randint(len(far))]
    return np.exp2(a.ravel()).repeat(32)


def f64(x):
    return np.asarray(x).astype(np.float64)


def striped(idx):
    return np.tile(np.asarray(idx).reshape(-1, 16).T, (8, 1)).astype(np.uint16)


def unstriped(offs):
    return offs[:16].T.reshape(-1).astype(np.int64)


E2M1 = np.array([0.0, 0.5, 1.0, 1.5, 2.0, 3.0, 4.0, 6.0, -0.0, -0.5, -1.0, -1.5, -2.0, -3.0, -4.0, -6.0])


def pack_weight(w, fmt):
    k, n = w.shape
    w = f64(np.asarray(w, np.float32).astype(ml_dtypes.bfloat16)).reshape(k // 32, 32, n)
    amax = np.abs(w).max(1)
    if fmt == "e4m3":
        byte = np.frexp(amax)[1] - 1 + 127 - 7
    else:
        mant, ex = np.frexp(amax / 6.0)
        byte = np.where(mant > 0.5, ex, ex - 1) + 127
    byte = np.clip(np.where(amax > 0, byte, 1), 1, 254)
    scaled = (w * np.exp2(127.0 - byte)[:, None, :]).reshape(k, n).astype(np.float32)
    by_word = np.ascontiguousarray(scaled.reshape(k // 512, 128, 4, n).transpose(0, 1, 3, 2))
    if fmt == "e4m3":
        words = by_word.astype(ml_dtypes.float8_e4m3fn).view(np.uint8)
    else:
        c = by_word.astype(ml_dtypes.float4_e2m1fn).view(np.uint8) & 0xF
        words = (c[..., 0::2] | (c[..., 1::2] << 4)).reshape(k // 512, 128, 2 * n)
    return np.ascontiguousarray(words), np.ascontiguousarray(byte.astype(np.uint8).reshape(k // 512, 16, n))


def unpack_weight(words, scales, fmt):
    g, _, n = scales.shape
    words = np.ascontiguousarray(words).reshape(g, 128, n, -1)
    if fmt == "e4m3":
        vals = words.view(ml_dtypes.float8_e4m3fn).astype(np.float64)
    else:
        nib = np.empty((g, 128, n, 4), np.uint8)
        nib[..., 0::2] = words & 0xF
        nib[..., 1::2] = words >> 4
        vals = E2M1[nib]
    vals = vals * np.repeat(np.exp2(scales.astype(np.float64) - 127.0), 8, axis=1)[..., None]
    return vals.transpose(0, 1, 3, 2).reshape(g * 512, n)


D, E, U, T, I, G, Q = 512, 512, 512, 2048, 512, 64, 128


def setup_inputs():
    n = np.random.standard_normal
    idx = np.random.permutation(T)[:I]
    idx2 = np.random.permutation(U)[:G]
    fd = mx_kscale(D)
    fe = mx_kscale(E)
    keysp = pack_weight(n((D, T)) / fd[:, None], "e4m3")
    valsp = pack_weight(n((E, T)) / fe[:, None], "e4m3")
    return {
        "pquery": (n((D, Q)) * 0.8 / np.sqrt(D) * fd[:, None]).astype(np.float32),
        "pgsum": (n((D, U)) / fd[:, None]).astype(np.float32),
        "query": (n((D, Q)) * 0.7 / np.sqrt(D) * fd[:, None]).astype(np.float32),
        "keys_words": keysp[0],
        "keys_scales": keysp[1],
        "gout": (n((E, Q)) * 1 / np.sqrt(E) * fe[:, None]).astype(np.float32),
        "pvals": (n((E, U)) * 0.7 / fe[:, None]).astype(np.float32),
        "vals_words": valsp[0],
        "vals_scales": valsp[1],
        "old": (0.5 * n((Q, U))).astype(np.float32),
        "offs": striped(idx),
        "offs2": striped(idx2),
    }


def reference(pquery, pgsum, query, keys_words, keys_scales, gout, pvals, vals_words, vals_scales, old, offs, offs2):
    idx = unstriped(offs)
    idx2 = unstriped(offs2)
    keysu = unpack_weight(keys_words, keys_scales, "e4m3")
    valsu = unpack_weight(vals_words, vals_scales, "e4m3")
    pqueryq = mxq(f64(pquery), 0, "e4m3")
    pgsumq = mxq(f64(pgsum), 0, "e4m3")
    b = pqueryq.T @ pgsumq
    m1 = np.max(b, axis=1, keepdims=True)
    pb = np.exp(b - m1)
    z = np.sum(pb, axis=1, keepdims=True)
    queryq = mxq(f64(query), 0, "e4m3")
    keysidxg = keysu[:, idx]
    a = queryq.T @ keysidxg
    pa = np.exp(a)
    s = pa.reshape(Q, G, I // G).sum(axis=2)
    mo = np.exp(b[:, idx2] - m1)
    sh = mo / s
    sr = np.repeat(sh, I // G, axis=1)
    goutq = mxq(f64(gout), 0, "e4m3")
    pvalsq = mxq(f64(pvals), 0, "e4m3")
    c0 = goutq.T @ pvalsq
    valsidxg = valsu[:, idx]
    c1 = goutq.T @ valsidxg
    dsr = 1.0 / z * c1 * pa
    dsh = dsr.reshape(Q, G, I // G).sum(axis=2)
    dmo = 1.0 / z * (-1.0) * c0[:, idx2] + dsh / s
    dz = (np.sum(pb * c0, axis=1, keepdims=True) - np.sum(mo * c0[:, idx2], axis=1, keepdims=True) + np.sum(pa * sr * c1, axis=1, keepdims=True)) / np.square(z) * (-1.0)
    dpb = 1.0 / z * c0 + dz
    e1 = dmo * mo
    s1 = np.zeros((Q, U))
    s1[:, idx2] = e1
    db = dpb * pb + s1
    y = db * 256.0 + f64(old)
    return y

@@ -1,0 +1,219 @@
+from contextlib import ExitStack
+
+import concourse.mybir as mybir
+from concourse.masks import make_identity
+
+F32 = mybir.dt.float32
+BF16 = mybir.dt.bfloat16
+I32 = mybir.dt.int32
+U32 = mybir.dt.uint32
+U16 = mybir.dt.uint16
+U8 = mybir.dt.uint8
+FP8X4 = mybir.dt.float8_e4m3fn_x4
+ALU = mybir.AluOpType
+ACT = mybir.ActivationFunctionType
+AX = mybir.AxisListType
+
+P = 128
+PACK = 4
+U, T, I, G, Q = 512, 2048, 512, 64, 128
+HALF = U // 2
+VALS_ROW = 4
+V_COLS = 256
+
+FLOPS = 4 * 2 * 512 * 128 * 512
+
+
+def load_rows(nc, pool, src, name):
+    width = src.shape[1]
+    raw = pool.tile([P, PACK, width], F32, name=name)
+    nc.sync.dma_start(out=raw[:], in_=src.rearrange("(p j) w -> p j w", j=PACK))
+    return raw
+
+
+def weave(copy, grouped, raw, c0, c1):
+    copy(
+        out=grouped[:, c0:c1, :].rearrange("p (c i) t -> p c t i", i=4),
+        in_=raw[:, :, c0:c1].rearrange("p t (c i) -> p c t i", i=4),
+    )
+
+
+def quantize(nc, pool, grouped, name):
+    width = grouped.shape[1]
+    codes = pool.tile([P, width], U32, name=name + "_codes", align_bytes=64)
+    scales = pool.tile([P, width], U8, name=name + "_scales", align_bytes=64)
+    nc.vector.quantize_mx(
+        out=codes[:].bitcast(FP8X4),
+        scales=scales[:],
+        in_=grouped[:].rearrange("p w j -> p (w j)"),
+    )
+    return codes, scales
+
+
+def product(nc, out, lhs, rhs_codes, rhs_scales):
+    nc.tensor.matmul_mx(
+        out=out,
+        lhsT=lhs[0].bitcast(FP8X4),
+        lhsT_scale=lhs[1],
+        rhs=rhs_codes.bitcast(FP8X4),
+        rhs_scale=rhs_scales,
+        start=True,
+        stop=True,
+    )
+
+
+def tile_attend_bopened_b_kernel(tc, pquery, pgsum, query, keys_words, keys_scales, gout, pvals,
+                                  vals_words, vals_scales, old, offs, offs2, out):
+    nc = tc.nc
+    with ExitStack() as ctx:
+        sb = ctx.enter_context(tc.tile_pool(name="sb", bufs=1))
+        ps = ctx.enter_context(tc.psum_pool(name="ps", bufs=1))
+
+        slots = sb.tile([P, I // 16], U16, name="slots")
+        pages = sb.tile([P, G // 16], U16, name="pages")
+        k_words = sb.tile([P, T], U32, name="k_words")
+        v_words = sb.tile([P, T], U32, name="v_words")
+        k_bytes = sb.tile([P, T], U8, name="k_bytes")
+        v_bytes = sb.tile([P, T], U8, name="v_bytes")
+        s1 = sb.tile([P, U], F32, name="s1")
+        old_sb = sb.tile([P, U], F32, name="old_sb")
+        ident = sb.tile([P, P], F32, name="ident")
+
+        nc.gpsimd.memset(k_bytes[:].bitcast(I32), 0)
+        nc.vector.memset(v_bytes[:].bitcast(I32), 0)
+        nc.vector.memset(s1[:], 0.0)
+        make_identity(nc, ident[:])
+
+        nc.sync.dma_start(slots[:], offs)
+        query_raw = load_rows(nc, sb, query, "query_raw")
+        gout_raw = load_rows(nc, sb, gout, "gout_raw")
+        pquery_raw = load_rows(nc, sb, pquery, "pquery_raw")
+        for quad in range(4):
+            nc.sync.dma_start(out=k_bytes[32 * quad:32 * quad + 4, :].bitcast(I32),
+                              in_=keys_scales[0, 4 * quad:4 * quad + 4, :].bitcast(I32))
+        nc.sync.dma_start(out=k_words[:].bitcast(I32),
+                          in_=keys_words[0].rearrange("p n t -> p (n t)").bitcast(I32))
+        for quad in range(4):
+            nc.sync.dma_start(out=v_bytes[32 * quad + VALS_ROW:32 * quad + VALS_ROW + 4, :].bitcast(I32),
+                              in_=vals_scales[0, 4 * quad:4 * quad + 4, :].bitcast(I32))
+        nc.sync.dma_start(out=v_words[:].bitcast(I32),
+                          in_=vals_words[0].rearrange("p n t -> p (n t)").bitcast(I32))
+        nc.sync.dma_start(pages[:], offs2)
+        pgsum_raw = [load_rows(nc, sb, pgsum[:, h * HALF:(h + 1) * HALF], "pgsum_raw%d" % h) for h in range(2)]
+        pvals_raw = [load_rows(nc, sb, pvals[:, h * HALF:(h + 1) * HALF], "pvals_raw%d" % h) for h in range(2)]
+        nc.sync.dma_start(out=old_sb[:], in_=old)
+
+        def woven(raw, name, v_cols):
+            width = raw.shape[2]
+            grouped = sb.tile([P, width, PACK], BF16, name=name + "_bf", align_bytes=64)
+            if v_cols > 0:
+                weave(nc.vector.tensor_copy, grouped, raw, 0, v_cols)
+            if v_cols < width:
+                weave(nc.scalar.copy, grouped, raw, v_cols, width)
+            codes, scales = quantize(nc, sb, grouped, name)
+            return codes[:], scales[:]
+
+        kg_bytes = sb.tile([P, I], U8, name="kg_bytes", align_bytes=64)
+        kg_words = sb.tile([P, I], U32, name="kg_words", align_bytes=64)
+        vg_bytes = sb.tile([P, I], U8, name="vg_bytes", align_bytes=64)
+        vg_words = sb.tile([P, I], U32, name="vg_words", align_bytes=64)
+        nc.vector.tensor_copy(kg_bytes[:], k_bytes[:].indirect(slots[:]))
+        query_q = woven(query_raw, "query", 0)
+        gout_q = woven(gout_raw, "gout", 0)
+        pquery_q = woven(pquery_raw, "pquery", 0)
+        nc.vector.tensor_copy(kg_words[:], k_words[:].indirect(slots[:]))
+        a_ps = ps.tile([P, I], F32, name="a_ps")
+        product(nc, a_ps[:], query_q, kg_words[:], kg_bytes[:])
+        terms = sb.tile([P, 8, 2, G], F32, name="terms")
+        nc.scalar.activation(out=terms[:, :, 0, :], in_=a_ps[:].rearrange("p (g j) -> p j g", j=8), func=ACT.Exp)
+
+        nc.vector.tensor_copy(vg_bytes[:], v_bytes[:].indirect(slots[:]))
+        nc.vector.tensor_copy(vg_words[:], v_words[:].indirect(slots[:]))
+        c1_ps = ps.tile([P, I], F32, name="c1_ps")
+        product(nc, c1_ps[:], gout_q, vg_words[:], vg_bytes[VALS_ROW:P, :])
+        nc.vector.tensor_tensor(terms[:, :, 1, :], c1_ps[:].rearrange("p (g j) -> p j g", j=8), terms[:, :, 0, :],
+                                ALU.mult)
+        sums_t_ps = ps.tile([P, P], F32, name="sums_t_ps")
+        for j in range(8):
+            nc.tensor.matmul(sums_t_ps[:], terms[:, j, :, :].rearrange("p h g -> p (h g)"), ident[:],
+                             is_transpose=True, start=(j == 0), stop=(j == 7))
+        sums_t = sb.tile([P, P], F32, name="sums_t")
+        nc.scalar.copy(out=sums_t[:], in_=sums_t_ps[:])
+        sums_ps = ps.tile([P, P], F32, name="sums_ps")
+        nc.tensor.transpose(sums_ps[:], sums_t[:], ident[:])
+
+        b_sb = sb.tile([P, U], F32, name="b_sb")
+        tops = sb.tile([P, 2], F32, name="tops")
+        for h in range(2):
+            pg_q = woven(pgsum_raw[h], "pgsum%d" % h, 0)
+            b_ps = ps.tile([P, HALF], F32, name="b_ps%d" % h)
+            product(nc, b_ps[:], pquery_q, pg_q[0], pg_q[1])
+            nc.vector.tensor_scalar(out=b_sb[:, h * HALF:(h + 1) * HALF], in0=b_ps[:], scalar1=1.0,
+                                    scalar2=tops[:, 0:1] if h else None,
+                                    op0=ALU.mult, op1=ALU.max, accum_out=tops[:, h:h + 1])
+        neg_m = sb.tile([P, 1], F32, name="neg_m")
+        nc.scalar.mul(neg_m[:], tops[:, 1:2], -1.0)
+        bg = sb.tile([P, G], F32, name="bg")
+        nc.vector.tensor_copy(bg[:], b_sb[:].indirect(pages[:]))
+        pb = sb.tile([P, U], F32, name="pb")
+        z = sb.tile([P, 1], F32, name="z")
+        nc.scalar.activation(out=pb[:], in_=b_sb[:], func=ACT.Exp, bias=neg_m[:], accum_out=z[:])
+        mo = sb.tile([P, G], F32, name="mo")
+        nc.scalar.activation(out=mo[:], in_=bg[:], func=ACT.Exp, bias=neg_m[:])
+
+        rs = sb.tile([P, G], F32, name="rs")
+        nc.vector.reciprocal(rs[:], sums_ps[:, 0:G])
+        mean1 = sb.tile([P, G], F32, name="mean1")
+        nc.vector.tensor_tensor(mean1[:], sums_ps[:, G:2 * G], rs[:], ALU.mult)
+
+        rz = sb.tile([P, 1], F32, name="rz")
+        nc.vector.reciprocal(rz[:], z[:])
+        neg_r = sb.tile([P, 1], F32, name="neg_r")
+        nc.scalar.mul(neg_r[:], rz[:], -256.0)
+        r_over_z = sb.tile([P, 1], F32, name="r_over_z")
+        nc.vector.tensor_scalar(out=r_over_z[:], in0=rz[:], scalar1=rz[:], scalar2=256.0, op0=ALU.mult, op1=ALU.mult)
+        parts = sb.tile([P, 2 * G + 2], F32, name="parts")
+        nc.vector.scalar_tensor_tensor(out=parts[:, G:2 * G], in0=mean1[:], scalar=-1.0, in1=mo[:],
+                                       op0=ALU.mult, op1=ALU.mult)
+
+        c0_sb = sb.tile([P, U], F32, name="c0_sb")
+        pc = sb.tile([P, U], F32, name="pc")
+        base = sb.tile([P, U], F32, name="base")
+        c0_ps = []
+        for h in range(2):
+            cols = slice(h * HALF, (h + 1) * HALF)
+            pv_q = woven(pvals_raw[h], "pvals%d" % h, V_COLS * h)
+            c0_ps.append(ps.tile([P, HALF], F32, name="c0_ps%d" % h))
+            product(nc, c0_ps[h][:], gout_q, pv_q[0], pv_q[1])
+            nc.scalar.copy(out=c0_sb[:, cols], in_=c0_ps[h][:])
+
+        def weigh(h):
+            cols = slice(h * HALF, (h + 1) * HALF)
+            nc.vector.scalar_tensor_tensor(out=pc[:, cols], in0=pb[:, cols], scalar=-1.0, in1=c0_ps[h][:],
+                                           op0=ALU.mult, op1=ALU.mult, accum_out=parts[:, 2 * G + h:2 * G + h + 1])
+
+        def add_old(h):
+            cols = slice(h * HALF, (h + 1) * HALF)
+            nc.vector.scalar_tensor_tensor(out=base[:, cols], in0=pc[:, cols], scalar=neg_r[:], in1=old_sb[:, cols],
+                                           op0=ALU.mult, op1=ALU.add)
+
+        weigh(0)
+        add_old(0)
+        nc.vector.tensor_tensor(parts[:, 0:G], c0_sb[:].indirect(pages[:]), mo[:], ALU.mult)
+        weigh(1)
+        nc.vector.tensor_tensor(s1[:].indirect(pages[:]), parts[:, 0:G], parts[:, G:2 * G], ALU.add)
+        add_old(1)
+        scaled = sb.tile([P, 2 * G + 2], F32, name="scaled")
+        w = sb.tile([P, 1], F32, name="w")
+        nc.scalar.activation(out=scaled[:], in_=parts[:], func=ACT.Identity, scale=r_over_z[:], accum_out=w[:])
+        mid = [sb.tile([P, HALF], F32, name="mid%d" % h) for h in range(2)]
+        for h in range(2):
+            cols = slice(h * HALF, (h + 1) * HALF)
+            nc.vector.scalar_tensor_tensor(out=mid[h][:], in0=s1[:, cols], scalar=neg_r[:], in1=base[:, cols],
+                                           op0=ALU.mult, op1=ALU.add)
+        for h in range(2):
+            cols = slice(h * HALF, (h + 1) * HALF)
+            res = sb.tile([P, HALF], F32, name="res%d" % h)
+            nc.vector.scalar_tensor_tensor(out=res[:], in0=pb[:, cols], scalar=w[:], in1=mid[h][:],
+                                           op0=ALU.mult, op1=ALU.add)
+            nc.sync.dma_start(out=out[:, cols], in_=res[:])

@@ -1,7 +1,6 @@
 from contextlib import ExitStack
 
 import concourse.mybir as mybir
-from concourse.masks import make_identity
 
 F32 = mybir.dt.float32
 BF16 = mybir.dt.bfloat16
@@ -19,22 +18,21 @@ PACK = 4
 U, T, I, G, Q = 512, 2048, 512, 64, 128
 HALF = U // 2
 VALS_ROW = 4
-V_COLS = 256
 
 FLOPS = 4 * 2 * 512 * 128 * 512
 
 
 def load_rows(nc, pool, src, name):
     width = src.shape[1]
-    raw = pool.tile([P, PACK, width], F32, name=name)
+    raw = pool.tile([P, PACK, width], F32, name=name, tag=name)
     nc.sync.dma_start(out=raw[:], in_=src.rearrange("(p j) w -> p j w", j=PACK))
     return raw
 
 
-def weave(copy, grouped, raw, c0, c1):
+def weave(copy, grouped, raw):
     copy(
-        out=grouped[:, c0:c1, :].rearrange("p (c i) t -> p c t i", i=4),
-        in_=raw[:, :, c0:c1].rearrange("p t (c i) -> p c t i", i=4),
+        out=grouped.rearrange("p (c i) t -> p c t i", i=4),
+        in_=raw.rearrange("p t (c i) -> p c t i", i=4),
     )
 
 
@@ -67,49 +65,47 @@ def tile_attend_bopened_b_kernel(tc, pquery, pgsum, query, keys_words, keys_scal
     nc = tc.nc
     with ExitStack() as ctx:
         sb = ctx.enter_context(tc.tile_pool(name="sb", bufs=1))
+        late = ctx.enter_context(tc.tile_pool(name="late", bufs=1))
         ps = ctx.enter_context(tc.psum_pool(name="ps", bufs=1))
 
         slots = sb.tile([P, I // 16], U16, name="slots")
         pages = sb.tile([P, G // 16], U16, name="pages")
         k_words = sb.tile([P, T], U32, name="k_words")
-        v_words = sb.tile([P, T], U32, name="v_words")
+        v_words = late.tile([P, T], U32, name="v_words", offset=0)
         k_bytes = sb.tile([P, T], U8, name="k_bytes")
         v_bytes = sb.tile([P, T], U8, name="v_bytes")
         s1 = sb.tile([P, U], F32, name="s1")
         old_sb = sb.tile([P, U], F32, name="old_sb")
-        ident = sb.tile([P, P], F32, name="ident")
 
         nc.gpsimd.memset(k_bytes[:].bitcast(I32), 0)
         nc.vector.memset(v_bytes[:].bitcast(I32), 0)
         nc.vector.memset(s1[:], 0.0)
-        make_identity(nc, ident[:])
+
+        def load_words(tile, words):
+            nc.sync.dma_start(out=tile[:].bitcast(I32), in_=words[0].rearrange("p n t -> p (n t)").bitcast(I32))
+
+        def load_bytes(tile, rows, first):
+            for quad in range(4):
+                nc.sync.dma_start(out=tile[32 * quad + first:32 * quad + first + 4, :].bitcast(I32),
+                                  in_=rows[0, 4 * quad:4 * quad + 4, :].bitcast(I32))
 
         nc.sync.dma_start(slots[:], offs)
         query_raw = load_rows(nc, sb, query, "query_raw")
-        gout_raw = load_rows(nc, sb, gout, "gout_raw")
+        load_bytes(k_bytes, keys_scales, 0)
+        load_words(k_words, keys_words)
+        load_bytes(v_bytes, vals_scales, VALS_ROW)
         pquery_raw = load_rows(nc, sb, pquery, "pquery_raw")
-        for quad in range(4):
-            nc.sync.dma_start(out=k_bytes[32 * quad:32 * quad + 4, :].bitcast(I32),
-                              in_=keys_scales[0, 4 * quad:4 * quad + 4, :].bitcast(I32))
-        nc.sync.dma_start(out=k_words[:].bitcast(I32),
-                          in_=keys_words[0].rearrange("p n t -> p (n t)").bitcast(I32))
-        for quad in range(4):
-            nc.sync.dma_start(out=v_bytes[32 * quad + VALS_ROW:32 * quad + VALS_ROW + 4, :].bitcast(I32),
-                              in_=vals_scales[0, 4 * quad:4 * quad + 4, :].bitcast(I32))
-        nc.sync.dma_start(out=v_words[:].bitcast(I32),
-                          in_=vals_words[0].rearrange("p n t -> p (n t)").bitcast(I32))
+        pgsum_raw = load_rows(nc, sb, pgsum, "pgsum_raw")
+        gout_raw = load_rows(nc, sb, gout, "gout_raw")
         nc.sync.dma_start(pages[:], offs2)
-        pgsum_raw = [load_rows(nc, sb, pgsum[:, h * HALF:(h + 1) * HALF], "pgsum_raw%d" % h) for h in range(2)]
-        pvals_raw = [load_rows(nc, sb, pvals[:, h * HALF:(h + 1) * HALF], "pvals_raw%d" % h) for h in range(2)]
+        pvals_raw = load_rows(nc, sb, pvals, "pvals_raw")
+        load_words(v_words, vals_words)
         nc.sync.dma_start(out=old_sb[:], in_=old)
 
-        def woven(raw, name, v_cols):
+        def woven(copy, raw, name):
             width = raw.shape[2]
-            grouped = sb.tile([P, width, PACK], BF16, name=name + "_bf", align_bytes=64)
-            if v_cols > 0:
-                weave(nc.vector.tensor_copy, grouped, raw, 0, v_cols)
-            if v_cols < width:
-                weave(nc.scalar.copy, grouped, raw, v_cols, width)
+            grouped = sb.tile([P, width, PACK], BF16, name=name + "_bf", tag=name + "_bf", align_bytes=64)
+            weave(copy, grouped[:], raw)
             codes, scales = quantize(nc, sb, grouped, name)
             return codes[:], scales[:]
 
@@ -117,93 +113,87 @@ def tile_attend_bopened_b_kernel(tc, pquery, pgsum, query, keys_words, keys_scal
         kg_words = sb.tile([P, I], U32, name="kg_words", align_bytes=64)
         vg_bytes = sb.tile([P, I], U8, name="vg_bytes", align_bytes=64)
         vg_words = sb.tile([P, I], U32, name="vg_words", align_bytes=64)
+        on_scalar, on_vector = nc.scalar.copy, nc.vector.tensor_copy
+        lo, hi = slice(0, HALF), slice(HALF, U)
+        query_q = woven(on_scalar, query_raw[:], "query")
         nc.vector.tensor_copy(kg_bytes[:], k_bytes[:].indirect(slots[:]))
-        query_q = woven(query_raw, "query", 0)
-        gout_q = woven(gout_raw, "gout", 0)
-        pquery_q = woven(pquery_raw, "pquery", 0)
         nc.vector.tensor_copy(kg_words[:], k_words[:].indirect(slots[:]))
         a_ps = ps.tile([P, I], F32, name="a_ps")
         product(nc, a_ps[:], query_q, kg_words[:], kg_bytes[:])
-        terms = sb.tile([P, 8, 2, G], F32, name="terms")
-        nc.scalar.activation(out=terms[:, :, 0, :], in_=a_ps[:].rearrange("p (g j) -> p j g", j=8), func=ACT.Exp)
-
         nc.vector.tensor_copy(vg_bytes[:], v_bytes[:].indirect(slots[:]))
-        nc.vector.tensor_copy(vg_words[:], v_words[:].indirect(slots[:]))
-        c1_ps = ps.tile([P, I], F32, name="c1_ps")
-        product(nc, c1_ps[:], gout_q, vg_words[:], vg_bytes[VALS_ROW:P, :])
-        nc.vector.tensor_tensor(terms[:, :, 1, :], c1_ps[:].rearrange("p (g j) -> p j g", j=8), terms[:, :, 0, :],
-                                ALU.mult)
-        sums_t_ps = ps.tile([P, P], F32, name="sums_t_ps")
-        for j in range(8):
-            nc.tensor.matmul(sums_t_ps[:], terms[:, j, :, :].rearrange("p h g -> p (h g)"), ident[:],
-                             is_transpose=True, start=(j == 0), stop=(j == 7))
-        sums_t = sb.tile([P, P], F32, name="sums_t")
-        nc.scalar.copy(out=sums_t[:], in_=sums_t_ps[:])
-        sums_ps = ps.tile([P, P], F32, name="sums_ps")
-        nc.tensor.transpose(sums_ps[:], sums_t[:], ident[:])
+        pquery_q = woven(on_scalar, pquery_raw[:], "pquery")
+        pa = sb.tile([P, I], F32, name="pa", tag="pquery_raw")
+        nc.scalar.activation(out=pa[:], in_=a_ps[:], func=ACT.Exp)
 
-        b_sb = sb.tile([P, U], F32, name="b_sb")
-        tops = sb.tile([P, 2], F32, name="tops")
-        for h in range(2):
-            pg_q = woven(pgsum_raw[h], "pgsum%d" % h, 0)
-            b_ps = ps.tile([P, HALF], F32, name="b_ps%d" % h)
-            product(nc, b_ps[:], pquery_q, pg_q[0], pg_q[1])
-            nc.vector.tensor_scalar(out=b_sb[:, h * HALF:(h + 1) * HALF], in0=b_ps[:], scalar1=1.0,
-                                    scalar2=tops[:, 0:1] if h else None,
-                                    op0=ALU.mult, op1=ALU.max, accum_out=tops[:, h:h + 1])
-        neg_m = sb.tile([P, 1], F32, name="neg_m")
-        nc.scalar.mul(neg_m[:], tops[:, 1:2], -1.0)
+        b_ps = ps.tile([P, U], F32, name="b_ps")
+        pg_hi = woven(on_vector, pgsum_raw[:, :, hi], "pgsum_hi")
+        product(nc, b_ps[:, hi], pquery_q, pg_hi[0], pg_hi[1])
+        s = sb.tile([P, G], F32, name="s", tag="pgsum_hi_bf", align_bytes=64)
+        nc.vector.tensor_reduce(out=s[:], in_=pa[:].rearrange("p (g j) -> p g j", j=8), axis=AX.X, op=ALU.add)
+        pg_lo = woven(on_scalar, pgsum_raw[:, :, lo], "pgsum_lo")
+        product(nc, b_ps[:, lo], pquery_q, pg_lo[0], pg_lo[1])
+        rs = sb.tile([P, G], F32, name="rs", tag="pgsum_lo_bf", align_bytes=64)
+        nc.vector.reciprocal(rs[:], s[:])
+        gout_q = woven(on_scalar, gout_raw[:], "gout")
+
+        c0_ps = ps.tile([P, U], F32, name="c0_ps")
+        pv_hi = woven(on_vector, pvals_raw[:, :, hi], "pvals_hi")
+        product(nc, c0_ps[:, hi], gout_q, pv_hi[0], pv_hi[1])
+        b_sb = sb.tile([P, U], F32, name="b_sb", tag="pvals_hi_bf", align_bytes=64)
+        top = sb.tile([P, 1], F32, name="top")
+        nc.vector.tensor_scalar(out=b_sb[:], in0=b_ps[:], scalar1=1.0, scalar2=None,
+                                op0=ALU.mult, op1=ALU.max, accum_out=top[:])
+        pv_lo = woven(on_scalar, pvals_raw[:, :, lo], "pvals_lo")
+        product(nc, c0_ps[:, lo], gout_q, pv_lo[0], pv_lo[1])
         bg = sb.tile([P, G], F32, name="bg")
         nc.vector.tensor_copy(bg[:], b_sb[:].indirect(pages[:]))
+
+        neg_m = sb.tile([P, 1], F32, name="neg_m")
+        nc.scalar.mul(neg_m[:], top[:], -1.0)
         pb = sb.tile([P, U], F32, name="pb")
         z = sb.tile([P, 1], F32, name="z")
         nc.scalar.activation(out=pb[:], in_=b_sb[:], func=ACT.Exp, bias=neg_m[:], accum_out=z[:])
         mo = sb.tile([P, G], F32, name="mo")
         nc.scalar.activation(out=mo[:], in_=bg[:], func=ACT.Exp, bias=neg_m[:])
 
-        rs = sb.tile([P, G], F32, name="rs")
-        nc.vector.reciprocal(rs[:], sums_ps[:, 0:G])
-        mean1 = sb.tile([P, G], F32, name="mean1")
-        nc.vector.tensor_tensor(mean1[:], sums_ps[:, G:2 * G], rs[:], ALU.mult)
-
-        rz = sb.tile([P, 1], F32, name="rz")
-        nc.vector.reciprocal(rz[:], z[:])
-        neg_r = sb.tile([P, 1], F32, name="neg_r")
-        nc.scalar.mul(neg_r[:], rz[:], -256.0)
-        r_over_z = sb.tile([P, 1], F32, name="r_over_z")
-        nc.vector.tensor_scalar(out=r_over_z[:], in0=rz[:], scalar1=rz[:], scalar2=256.0, op0=ALU.mult, op1=ALU.mult)
-        parts = sb.tile([P, 2 * G + 2], F32, name="parts")
-        nc.vector.scalar_tensor_tensor(out=parts[:, G:2 * G], in0=mean1[:], scalar=-1.0, in1=mo[:],
-                                       op0=ALU.mult, op1=ALU.mult)
-
-        c0_sb = sb.tile([P, U], F32, name="c0_sb")
-        pc = sb.tile([P, U], F32, name="pc")
-        base = sb.tile([P, U], F32, name="base")
-        c0_ps = []
+        c1_ps = []
         for h in range(2):
             cols = slice(h * HALF, (h + 1) * HALF)
-            pv_q = woven(pvals_raw[h], "pvals%d" % h, V_COLS * h)
-            c0_ps.append(ps.tile([P, HALF], F32, name="c0_ps%d" % h))
-            product(nc, c0_ps[h][:], gout_q, pv_q[0], pv_q[1])
-            nc.scalar.copy(out=c0_sb[:, cols], in_=c0_ps[h][:])
-
-        def weigh(h):
+            nc.vector.tensor_copy(vg_words[:, cols], v_words[:].indirect(slots[:, 16 * h:16 * (h + 1)]))
+            c1_ps.append(ps.tile([P, HALF], F32, name="c1_ps%d" % h))
+            product(nc, c1_ps[h][:], gout_q, vg_words[:, cols], vg_bytes[VALS_ROW:P, cols])
+        rz = late.tile([P, 1], F32, name="rz", offset=4096)
+        pc = late.tile([P, U], F32, name="pc", offset=0)
+        share = late.tile([P, G], F32, name="share", offset=4352)
+        parts = late.tile([P, 2 * G + 1], F32, name="parts", offset=5120)
+        neg_r = sb.tile([P, 1], F32, name="neg_r")
+        r_over_z = sb.tile([P, 1], F32, name="r_over_z")
+        base = sb.tile([P, U], F32, name="base")
+        c0_sb = sb.tile([P, U], F32, name="c0_sb")
+        c1pa = sb.tile([P, I], F32, name="c1pa")
+        rsum = sb.tile([P, G], F32, name="rsum")
+        nc.vector.scalar_tensor_tensor(out=pc[:], in0=pb[:], scalar=-1.0, in1=c0_ps[:],
+                                       op0=ALU.mult, op1=ALU.mult, accum_out=parts[:, 2 * G:2 * G + 1])
+        nc.scalar.copy(out=c0_sb[:], in_=c0_ps[:])
+        for h in range(2):
             cols = slice(h * HALF, (h + 1) * HALF)
-            nc.vector.scalar_tensor_tensor(out=pc[:, cols], in0=pb[:, cols], scalar=-1.0, in1=c0_ps[h][:],
-                                           op0=ALU.mult, op1=ALU.mult, accum_out=parts[:, 2 * G + h:2 * G + h + 1])
-
-        def add_old(h):
+            nc.vector.tensor_tensor(c1pa[:, cols], c1_ps[h][:], pa[:, cols], ALU.mult)
+        nc.vector.reciprocal(rz[:], z[:])
+        nc.scalar.mul(neg_r[:], rz[:], -256.0)
+        nc.scalar.activation(out=r_over_z[:], in_=rz[:], func=ACT.Square, scale=16.0)
+        for h in range(2):
+            cols = slice(h * HALF, (h + 1) * HALF)
+            nc.vector.tensor_reduce(out=rsum[:, 32 * h:32 * (h + 1)],
+                                    in_=c1pa[:, cols].rearrange("p (g j) -> p g j", j=8), axis=AX.X, op=ALU.add)
+        nc.vector.scalar_tensor_tensor(out=share[:], in0=mo[:], scalar=-1.0, in1=rs[:], op0=ALU.mult, op1=ALU.mult)
+        nc.vector.tensor_tensor(parts[:, 0:G], c0_sb[:].indirect(pages[:]), mo[:], ALU.mult)
+        nc.vector.tensor_tensor(parts[:, G:2 * G], rsum[:], share[:], ALU.mult)
+        nc.vector.tensor_tensor(s1[:].indirect(pages[:]), parts[:, 0:G], parts[:, G:2 * G], ALU.add)
+        for h in range(2):
             cols = slice(h * HALF, (h + 1) * HALF)
             nc.vector.scalar_tensor_tensor(out=base[:, cols], in0=pc[:, cols], scalar=neg_r[:], in1=old_sb[:, cols],
                                            op0=ALU.mult, op1=ALU.add)
-
-        weigh(0)
-        add_old(0)
-        nc.vector.tensor_tensor(parts[:, 0:G], c0_sb[:].indirect(pages[:]), mo[:], ALU.mult)
-        weigh(1)
-        nc.vector.tensor_tensor(s1[:].indirect(pages[:]), parts[:, 0:G], parts[:, G:2 * G], ALU.add)
-        add_old(1)
-        scaled = sb.tile([P, 2 * G + 2], F32, name="scaled")
+        scaled = sb.tile([P, 2 * G + 1], F32, name="scaled")
         w = sb.tile([P, 1], F32, name="w")
         nc.scalar.activation(out=scaled[:], in_=parts[:], func=ACT.Identity, scale=r_over_z[:], accum_out=w[:])
         mid = [sb.tile([P, HALF], F32, name="mid%d" % h) for h in range(2)]

from contextlib import ExitStack

import concourse.mybir as mybir

F32 = mybir.dt.float32
BF16 = mybir.dt.bfloat16
I32 = mybir.dt.int32
U32 = mybir.dt.uint32
U16 = mybir.dt.uint16
U8 = mybir.dt.uint8
FP8X4 = mybir.dt.float8_e4m3fn_x4
ALU = mybir.AluOpType
ACT = mybir.ActivationFunctionType
AX = mybir.AxisListType

P = 128
PACK = 4
U, T, I, G, Q = 512, 2048, 512, 64, 128
HALF = U // 2
VALS_ROW = 4

FLOPS = 4 * 2 * 512 * 128 * 512


def load_rows(nc, pool, src, name):
    width = src.shape[1]
    raw = pool.tile([P, PACK, width], F32, name=name, tag=name)
    nc.sync.dma_start(out=raw[:], in_=src.rearrange("(p j) w -> p j w", j=PACK))
    return raw


def weave(copy, grouped, raw):
    copy(
        out=grouped.rearrange("p (c i) t -> p c t i", i=4),
        in_=raw.rearrange("p t (c i) -> p c t i", i=4),
    )


def quantize(nc, pool, grouped, name):
    width = grouped.shape[1]
    codes = pool.tile([P, width], U32, name=name + "_codes", align_bytes=64)
    scales = pool.tile([P, width], U8, name=name + "_scales", align_bytes=64)
    nc.vector.quantize_mx(
        out=codes[:].bitcast(FP8X4),
        scales=scales[:],
        in_=grouped[:].rearrange("p w j -> p (w j)"),
    )
    return codes, scales


def product(nc, out, lhs, rhs_codes, rhs_scales):
    nc.tensor.matmul_mx(
        out=out,
        lhsT=lhs[0].bitcast(FP8X4),
        lhsT_scale=lhs[1],
        rhs=rhs_codes.bitcast(FP8X4),
        rhs_scale=rhs_scales,
        start=True,
        stop=True,
    )


def tile_attend_bopened_b_kernel(tc, pquery, pgsum, query, keys_words, keys_scales, gout, pvals,
                                  vals_words, vals_scales, old, offs, offs2, out):
    nc = tc.nc
    with ExitStack() as ctx:
        sb = ctx.enter_context(tc.tile_pool(name="sb", bufs=1))
        late = ctx.enter_context(tc.tile_pool(name="late", bufs=1))
        ps = ctx.enter_context(tc.psum_pool(name="ps", bufs=1))

        slots = sb.tile([P, I // 16], U16, name="slots")
        pages = sb.tile([P, G // 16], U16, name="pages")
        k_words = sb.tile([P, T], U32, name="k_words")
        v_words = late.tile([P, T], U32, name="v_words", offset=0)
        k_bytes = sb.tile([P, T], U8, name="k_bytes")
        v_bytes = sb.tile([P, T], U8, name="v_bytes")
        s1 = sb.tile([P, U], F32, name="s1")
        old_sb = sb.tile([P, U], F32, name="old_sb")

        nc.gpsimd.memset(k_bytes[:].bitcast(I32), 0)
        nc.vector.memset(v_bytes[:].bitcast(I32), 0)
        nc.vector.memset(s1[:], 0.0)

        def load_words(tile, words):
            nc.sync.dma_start(out=tile[:].bitcast(I32), in_=words[0].rearrange("p n t -> p (n t)").bitcast(I32))

        def load_bytes(tile, rows, first):
            for quad in range(4):
                nc.sync.dma_start(out=tile[32 * quad + first:32 * quad + first + 4, :].bitcast(I32),
                                  in_=rows[0, 4 * quad:4 * quad + 4, :].bitcast(I32))

        nc.sync.dma_start(slots[:], offs)
        query_raw = load_rows(nc, sb, query, "query_raw")
        load_bytes(k_bytes, keys_scales, 0)
        load_words(k_words, keys_words)
        load_bytes(v_bytes, vals_scales, VALS_ROW)
        pquery_raw = load_rows(nc, sb, pquery, "pquery_raw")
        pgsum_raw = load_rows(nc, sb, pgsum, "pgsum_raw")
        gout_raw = load_rows(nc, sb, gout, "gout_raw")
        nc.sync.dma_start(pages[:], offs2)
        pvals_raw = load_rows(nc, sb, pvals, "pvals_raw")
        load_words(v_words, vals_words)
        nc.sync.dma_start(out=old_sb[:], in_=old)

        def woven(copy, raw, name):
            width = raw.shape[2]
            grouped = sb.tile([P, width, PACK], BF16, name=name + "_bf", tag=name + "_bf", align_bytes=64)
            weave(copy, grouped[:], raw)
            codes, scales = quantize(nc, sb, grouped, name)
            return codes[:], scales[:]

        kg_bytes = sb.tile([P, I], U8, name="kg_bytes", align_bytes=64)
        kg_words = sb.tile([P, I], U32, name="kg_words", align_bytes=64)
        vg_bytes = sb.tile([P, I], U8, name="vg_bytes", align_bytes=64)
        vg_words = sb.tile([P, I], U32, name="vg_words", align_bytes=64)
        on_scalar, on_vector = nc.scalar.copy, nc.vector.tensor_copy
        lo, hi = slice(0, HALF), slice(HALF, U)
        query_q = woven(on_scalar, query_raw[:], "query")
        nc.vector.tensor_copy(kg_bytes[:], k_bytes[:].indirect(slots[:]))
        nc.vector.tensor_copy(kg_words[:], k_words[:].indirect(slots[:]))
        a_ps = ps.tile([P, I], F32, name="a_ps")
        product(nc, a_ps[:], query_q, kg_words[:], kg_bytes[:])
        nc.vector.tensor_copy(vg_bytes[:], v_bytes[:].indirect(slots[:]))
        pquery_q = woven(on_scalar, pquery_raw[:], "pquery")
        pa = sb.tile([P, I], F32, name="pa", tag="pquery_raw")
        nc.scalar.activation(out=pa[:], in_=a_ps[:], func=ACT.Exp)

        b_ps = ps.tile([P, U], F32, name="b_ps")
        pg_hi = woven(on_vector, pgsum_raw[:, :, hi], "pgsum_hi")
        product(nc, b_ps[:, hi], pquery_q, pg_hi[0], pg_hi[1])
        s = sb.tile([P, G], F32, name="s", tag="pgsum_hi_bf", align_bytes=64)
        nc.vector.tensor_reduce(out=s[:], in_=pa[:].rearrange("p (g j) -> p g j", j=8), axis=AX.X, op=ALU.add)
        pg_lo = woven(on_scalar, pgsum_raw[:, :, lo], "pgsum_lo")
        product(nc, b_ps[:, lo], pquery_q, pg_lo[0], pg_lo[1])
        rs = sb.tile([P, G], F32, name="rs", tag="pgsum_lo_bf", align_bytes=64)
        nc.vector.reciprocal(rs[:], s[:])
        gout_q = woven(on_scalar, gout_raw[:], "gout")

        c0_ps = ps.tile([P, U], F32, name="c0_ps")
        pv_hi = woven(on_vector, pvals_raw[:, :, hi], "pvals_hi")
        product(nc, c0_ps[:, hi], gout_q, pv_hi[0], pv_hi[1])
        b_sb = sb.tile([P, U], F32, name="b_sb", tag="pvals_hi_bf", align_bytes=64)
        top = sb.tile([P, 1], F32, name="top")
        nc.vector.tensor_scalar(out=b_sb[:], in0=b_ps[:], scalar1=1.0, scalar2=None,
                                op0=ALU.mult, op1=ALU.max, accum_out=top[:])
        pv_lo = woven(on_scalar, pvals_raw[:, :, lo], "pvals_lo")
        product(nc, c0_ps[:, lo], gout_q, pv_lo[0], pv_lo[1])
        bg = sb.tile([P, G], F32, name="bg")
        nc.vector.tensor_copy(bg[:], b_sb[:].indirect(pages[:]))

        neg_m = sb.tile([P, 1], F32, name="neg_m")
        nc.scalar.mul(neg_m[:], top[:], -1.0)
        pb = sb.tile([P, U], F32, name="pb")
        z = sb.tile([P, 1], F32, name="z")
        nc.scalar.activation(out=pb[:], in_=b_sb[:], func=ACT.Exp, bias=neg_m[:], accum_out=z[:])
        mo = sb.tile([P, G], F32, name="mo")
        nc.scalar.activation(out=mo[:], in_=bg[:], func=ACT.Exp, bias=neg_m[:])

        c1_ps = []
        for h in range(2):
            cols = slice(h * HALF, (h + 1) * HALF)
            nc.vector.tensor_copy(vg_words[:, cols], v_words[:].indirect(slots[:, 16 * h:16 * (h + 1)]))
            c1_ps.append(ps.tile([P, HALF], F32, name="c1_ps%d" % h))
            product(nc, c1_ps[h][:], gout_q, vg_words[:, cols], vg_bytes[VALS_ROW:P, cols])
        rz = late.tile([P, 1], F32, name="rz", offset=4096)
        pc = late.tile([P, U], F32, name="pc", offset=0)
        share = late.tile([P, G], F32, name="share", offset=4352)
        parts = late.tile([P, 2 * G + 1], F32, name="parts", offset=5120)
        neg_r = sb.tile([P, 1], F32, name="neg_r")
        r_over_z = sb.tile([P, 1], F32, name="r_over_z")
        base = sb.tile([P, U], F32, name="base")
        c0_sb = sb.tile([P, U], F32, name="c0_sb")
        c1pa = sb.tile([P, I], F32, name="c1pa")
        rsum = sb.tile([P, G], F32, name="rsum")
        nc.vector.scalar_tensor_tensor(out=pc[:], in0=pb[:], scalar=-1.0, in1=c0_ps[:],
                                       op0=ALU.mult, op1=ALU.mult, accum_out=parts[:, 2 * G:2 * G + 1])
        nc.scalar.copy(out=c0_sb[:], in_=c0_ps[:])
        for h in range(2):
            cols = slice(h * HALF, (h + 1) * HALF)
            nc.vector.tensor_tensor(c1pa[:, cols], c1_ps[h][:], pa[:, cols], ALU.mult)
        nc.vector.reciprocal(rz[:], z[:])
        nc.scalar.mul(neg_r[:], rz[:], -256.0)
        nc.scalar.activation(out=r_over_z[:], in_=rz[:], func=ACT.Square, scale=16.0)
        for h in range(2):
            cols = slice(h * HALF, (h + 1) * HALF)
            nc.vector.tensor_reduce(out=rsum[:, 32 * h:32 * (h + 1)],
                                    in_=c1pa[:, cols].rearrange("p (g j) -> p g j", j=8), axis=AX.X, op=ALU.add)
        nc.vector.scalar_tensor_tensor(out=share[:], in0=mo[:], scalar=-1.0, in1=rs[:], op0=ALU.mult, op1=ALU.mult)
        nc.vector.tensor_tensor(parts[:, 0:G], c0_sb[:].indirect(pages[:]), mo[:], ALU.mult)
        nc.vector.tensor_tensor(parts[:, G:2 * G], rsum[:], share[:], ALU.mult)
        nc.vector.tensor_tensor(s1[:].indirect(pages[:]), parts[:, 0:G], parts[:, G:2 * G], ALU.add)
        for h in range(2):
            cols = slice(h * HALF, (h + 1) * HALF)
            nc.vector.scalar_tensor_tensor(out=base[:, cols], in0=pc[:, cols], scalar=neg_r[:], in1=old_sb[:, cols],
                                           op0=ALU.mult, op1=ALU.add)
        scaled = sb.tile([P, 2 * G + 1], F32, name="scaled")
        w = sb.tile([P, 1], F32, name="w")
        nc.scalar.activation(out=scaled[:], in_=parts[:], func=ACT.Identity, scale=r_over_z[:], accum_out=w[:])
        mid = [sb.tile([P, HALF], F32, name="mid%d" % h) for h in range(2)]
        for h in range(2):
            cols = slice(h * HALF, (h + 1) * HALF)
            nc.vector.scalar_tensor_tensor(out=mid[h][:], in0=s1[:, cols], scalar=neg_r[:], in1=base[:, cols],
                                           op0=ALU.mult, op1=ALU.add)
        for h in range(2):
            cols = slice(h * HALF, (h + 1) * HALF)
            res = sb.tile([P, HALF], F32, name="res%d" % h)
            nc.vector.scalar_tensor_tensor(out=res[:], in0=pb[:, cols], scalar=w[:], in1=mid[h][:],
                                           op0=ALU.mult, op1=ALU.add)
            nc.sync.dma_start(out=out[:, cols], in_=res[:])
